import numpy as np, ml_dtypes
CORES = [48,51,52,55]
N = 4
import mx_ref
BF = ml_dtypes.bfloat16
def gcols(t, e):
    v = np.concatenate([t.reshape(8, 16, -1, 4), np.zeros((8, 16, 1, 4), BF)], axis=2)
    return np.ascontiguousarray(np.stack([v[g][:, e[g]] for g in range(8)])).reshape(128, -1)
def tile(rs):
    return np.stack(rs, axis=2).reshape(128, -1).astype(BF)
def pick(q, e):
    c = np.concatenate([q[0].reshape(128, -1, 4), np.zeros((128, 1, 4), np.uint8)], axis=1); s = np.concatenate([q[1], np.ones((16, 1), np.uint8)], axis=1)
    return (np.ascontiguousarray(c[:, e].reshape(128, -1)), np.ascontiguousarray(s[:, e]))
def join(*qs):
    return (np.concatenate([q[0] for q in qs], axis=1), np.concatenate([q[1] for q in qs], axis=1))
def put(q, e, v):
    c, s = q[0].reshape(128, -1, 4).copy(), q[1].copy(); c[:, e] = v[0].reshape(128, -1, 4); s[:, e] = v[1]
    return (c.reshape(128, -1), s)
def pk(c, s):
    return (np.ascontiguousarray(c), mx_ref.live(s))
def emit(q):
    return q[0], q[1]
def packed(v, rng):
    q = [mx_ref.quantize(np.ascontiguousarray(v[r])) for r in range(N)]
    return np.stack([a for a, b in q]), np.stack([mx_ref.plane(b, rng) for a, b in q])
def values_of_codes():
    e, c = np.zeros((128, 128, 4), np.float32), np.zeros((128, 2, 4), np.uint8)
    e[np.arange(128), np.arange(128), 0] = 1
    c[:127, :, 0] = np.arange(256).reshape(2, 128).T[:127]
    return mx_ref.matmul(mx_ref.quantize(e.reshape(128, 512).astype(BF)), (c.reshape(128, 8), np.full((16, 2), 127, np.uint8))).T.reshape(-1).astype(np.float64)
CODE_VALUE, SCALE_VALUE = values_of_codes(), 2.0 ** (np.arange(256) - 127.0)
def decode(q):
    return (CODE_VALUE[q[0]].reshape(16, 8, -1, 4) * SCALE_VALUE[q[1]][:, None, :, None] + 0.0).reshape(128, -1).astype(np.float32)
def f(rng, *shape):
    return mx_ref.flush((rng.standard_normal(shape, dtype=np.float32) * np.exp2(rng.integers(-2, 3, shape[:-1] + (1,)))).astype(BF))
def wide(rng, *shape, cols=0):
    v = rng.standard_normal(shape, dtype=np.float32) * np.exp2(rng.integers(-12, 13, shape)).astype(np.float32)
    if cols: v *= np.repeat(np.exp2(rng.integers(-cols, cols + 1, shape[:-2] + (1, shape[-1] // 4))) * (rng.random(shape[:-2] + (1, shape[-1] // 4)) > 0.0625), 4, axis=-1).astype(np.float32)
    return mx_ref.flush(v.astype(BF))
C, K, R = 320, 64, 3
STEP = [1, 2, 3]
def order(p):
    return np.argsort(-(p[::16] + np.float32(0.0)), axis=1, kind="stable")
def big(v):
    v = v.astype(np.float32)
    v[np.abs(v) < np.float32(2.0 ** -16)] = 0
    return v.astype(BF)
def numbers_of(rng):
    return {"x": big(f(rng, N, 128, 4 * C)), "u": np.array(f(rng, N, 128, 512)), "v": np.array(f(rng, N, 128, 512))}
def layers(rng, still=0):
    w = big(f(rng, N, 128, 2048)).reshape(N, 8, 16, 4, 8, 16, 4)
    w[:, :, :still] = 0
    w[:, :, :, :, :, :still] = 0
    return w
def weights(rng, w):
    c, p = packed(np.ascontiguousarray(w).reshape(N, 128, 2048), rng)
    return {"wc": c, "ws": p}
def signs(rng):
    return np.stack([rng.permutation(8) % 2 * 2.0 - 1.0 for r in range(N)])
def setup_inputs(rng):
    return {**numbers_of(rng), **weights(rng, layers(rng))}
def setup_inputs_ties(rng):
    d = numbers_of(rng)
    e = rng.permutation(N)
    x = d["x"].reshape(N, 8, 16, C, 4)
    for r in range(N):
        k = np.zeros(C, int) if r == e[0] else rng.permutation(C) % 3
        a = x[r][:, :8, :3].copy()
        a[:, :, 2] = 0
        x[r][:, :8] = a[:, :, k]
    x[e[1]] = 0
    u = d["u"].reshape(N, 8, 16, 8, 16, 4)
    k = u.copy()
    u[:, :, :, :, :4] = 0
    for g in range(8): u[:, g, :8, g, :4] = k[:, g, :8, g, :4]
    return {"x": x.reshape(N, 128, 4 * C), "u": u.reshape(N, 128, 512), "v": d["v"], **weights(rng, layers(rng, 8))}
def setup_inputs_near(rng):
    d = numbers_of(rng)
    x = np.zeros((N, 8, 16, C, 4), np.float32)
    d["u"].reshape(N, 128, 8, 16, 4)[:, :, :, :4] = 0
    u = d["u"].reshape(N, 128, 128, 4)
    o, c = rng.permutation(N) % 4, signs(rng)
    upper = np.arange(C) // (C // 2)
    for r in range(N):
        i = (np.arange(C) + rng.integers(0, C, (8, 1))) % C
        if o[r] == 3: i = i % (C // 2) * 2 + upper
        s = (i + 1) // 2
        size = 1.0 if o[r] < 2 else 2.0 ** -4
        z = ((s[:, :, None] >> np.arange(8)) & 1) * np.exp2(np.arange(8) - 23.0) * size
        if o[r] < 2: x[r, :, 0, :, 0] = c[r][:, None]
        if o[r] == 1:
            for g in rng.permutation(8)[:4]: x[r, g, 0, rng.integers(C), 0] *= np.float32(2.0 ** 30)
        if o[r] == 3: x[r, :, 0, :, 0] = (8 + upper) * 2.0 ** -30
        a = rng.integers(-1, 2, (8, 3, C))
        if o[r] < 2: x[r, :, 1:4, :, 0] = a
        else:
            x[r, :, 1:4, :, 0] = (5 * a * a + a) * 2.0 ** -31
            x[r, :, 1:4, :, 1] = (a - 5 * a * a) * 2.0 ** -31
        x[r, :, 8] = z[:, :, :4]
        x[r, :, 9] = z[:, :, 4:]
        x[r, :, 10:] = rng.integers(4, 8, (8, 6, C, 4)) * 2.0 ** -20 * size
        k = 1.0 if o[r] == 0 else 2.0 ** -30
        for h in range(0, 128, 16):
            for n in range(4): u[r, h + n, h + n, :2] = k
            u[r, h + 8:h + 10, h] = k
    w = np.abs(layers(rng, 10).astype(np.float32)) * np.float32(2.0 ** -6)
    return {"x": x.reshape(N, 128, 4 * C).astype(BF), "u": u.reshape(N, 128, 512), "v": d["v"], **weights(rng, w.astype(BF))}
def setup_inputs_huge(rng):
    d = numbers_of(rng)
    c = np.stack([rng.permutation(C) % 2 * 2.0 - 1.0 for r in range(N)])
    c[rng.permutation(N) < N // 2] = -1
    x = 2.0 ** 30 * (0.75 + 0.13 * rng.random((N, 128, C, 4))) * c[:, None, :, None]
    s = np.stack([signs(rng) for i in range(4)], axis=2)
    a = 2.0 ** 30 * (1 - 0.25 * rng.random((N, 128, 8, 4, 4))) * s[:, None, :, :, None]
    d["u"].reshape(N, 128, 8, 16, 4)[:, :, :, :4] = a.astype(np.float32).astype(BF)
    w = np.zeros((N, 128, 4, 128, 4), np.float32)
    i = np.arange(128)
    for b in range(4): w[:, i, b, i, b] = -1
    return {"x": x.astype(np.float32).reshape(N, 128, 4 * C).astype(BF), "u": d["u"], "v": d["v"], **weights(rng, w.astype(BF))}
def setup_inputs_votes(rng):
    d = numbers_of(rng)
    x = d["x"].reshape(N, 8, 16, C, 4)
    x[:, :, :8] = 0
    kinds = rng.permutation(8)
    for g in range(8):
        e0, a0 = rng.permutation(C)[:K], rng.integers(0, 8, C)
        s0, q = int(rng.integers(C - K + 1)), int(rng.integers(1, C // 16))
        for r in range(N):
            e, a = rng.permutation(C)[:K], rng.integers(0, 8, C)
            if kinds[g] == 0: a[:] = r
            if kinds[g] == 1:
                e = (np.arange(K) + rng.integers(C)) % C
                a[:] = 7
            if kinds[g] == 2:
                e = rng.permutation(C // 2)[:K // 2]
                e, a = np.concatenate([e, e + C // 2]), np.tile(a[:C // 2], 2)
            if kinds[g] == 3:
                s = 16 * int(rng.integers(C // 16)) + int(rng.integers(2))
                e, a = (e0 + s) % C, np.roll(a0, s)
            if kinds[g] == 4: e = np.arange(K)
            if kinds[g] == 5: e = np.arange(C - K, C)
            if kinds[g] == 6:
                e = (s0 - 16 * q * (1 - r % 2) + np.arange(K)) % C
                if r % 2 == 0: e[1] = (s0 - 16 * q + K + 16) % C
                a[:] = 7
            p = -1.0 * rng.integers(0, 2, C)
            p[e] = 1 + 0.125 * rng.integers(0, 8, K)
            x[r, g, 0, :, 0] = p.astype(BF)
            for i in range(3): x[r, g, 1 + i, :, 0] = np.where((a >> i) & 1 == 1, 1.0, -1.0 * rng.integers(0, 2, C)).astype(BF)
    d["u"].reshape(N, 128, 8, 16, 4)[:, :, :, :4] = 0
    u = d["u"].reshape(N, 128, 128, 4)
    for h in range(0, 128, 16):
        for n in range(4): u[:, h + n, h + n, 0] = 1
    return {"x": x.reshape(N, 128, 4 * C), "u": u.reshape(N, 128, 512), "v": d["v"], **weights(rng, layers(rng, 8))}
def setup_inputs_spread(rng):
    d = setup_inputs(rng)
    d["x"] = big(wide(rng, N, 128, 4 * C, cols=6))
    return d
def check_inputs(d):
    b = []
    for k in ("x", "u", "v"):
        a = np.abs(d[k].astype(np.float32))
        if not (np.isfinite(a).all() and ((a == 0) | (a >= 2.0 ** -30) & (a <= 2.0 ** 30)).all()): b.append("a value of " + k)
    none, least, most = [emit(mx_ref.quantize(np.full((128, 16), k, np.float32).astype(BF)))[1][0, 0] for k in (0.0, 2.0 ** -30, 2.0 ** 30)]
    for r in range(N):
        if ((d["wc"][r] == 0x7F) | (d["wc"][r] == 0xFF)).any(): b.append("wc: a code that is no number")
        s = mx_ref.live(d["ws"][r])
        if ((s != none) & ((s < least) | (s > most))).any(): b.append("ws: a scale out of range")
    return b
def reference(x, u, v, wc, ws):
    qu = [mx_ref.quantize(u[r]) for r in range(N)]
    lay = [pk(wc[r], ws[r]) for r in range(N)]
    now = [x[r] for r in range(N)]
    y, ol = np.zeros((N, 128, C), np.float32), np.zeros((N, 8, C), np.float32)
    oc, osc = np.zeros((N, 128, 4 * C), np.uint8), np.zeros((N, 16, C), np.uint8)
    for t in range(R):
        came, peak, key = [], [], []
        for r in range(N):
            p = mx_ref.matmul(qu[r], mx_ref.quantize(now[r]))
            e = np.sort(order(p)[:, :K], axis=1)
            a = np.take_along_axis((p[1::16] > 0) + 2 * (p[2::16] > 0) + 4 * (p[3::16] > 0), e, axis=1)
            peak.append(e)
            key.append(a + 8 * np.roll(a, -1, axis=1))
            came.append(decode(mx_ref.quantize(gcols(now[r], e))))
        made = []
        for r in range(N):
            o = (r + STEP[t]) % N
            at = (peak[o][:, None, :] - peak[r][:, :, None]) % C // 16
            same = key[o][:, None, :] == key[r][:, :, None]
            shift = np.array([16 * np.argmax(np.bincount(at[g][same[g]], minlength=C // 16)) for g in range(8)])
            place = (np.arange(C) + shift[:, None]) % C
            m = np.sum(peak[o][:, None, :] <= place[:, :, None], axis=2) - 1
            m = np.where(m < 0, K - 1, m)
            ol[r] = np.take_along_axis(peak[o], m, axis=1)
            own = now[r].astype(np.float32)
            z = ((own + gcols(came[o].astype(BF), m).astype(np.float32)) * np.float32(0.5)).astype(BF)
            q = mx_ref.quantize(z)
            made.append(tile([mx_ref.matmul(pick(lay[r], np.arange(128 * b, 128 * b + 128)), q) * np.float32(0.03125) + own[:, b::4] for b in range(4)]))
        now = made
    for r in range(N):
        q = mx_ref.quantize(now[r])
        y[r] = mx_ref.matmul(mx_ref.quantize(v[r]), q)
        oc[r], osc[r] = emit(q)
    return {"y": y, "ol": ol, "oc": oc, "osc": osc}

import numpy as np
from concourse.mybir import dt, AluOpType, AxisListType, ActivationFunctionType

C, K, R = 320, 64, 3
STEP = [1, 2, 3]
NA = 190
ND = C - NA
HD = ND // 2
NP = C - 3 * 16
NV = 42
VA = 72
VD = (128 - VA) // 2
HA = 176
KK = 1024.0
BIG = 1.0e9
F32, BF, I32, U16, Q4, U8 = "float32", "bfloat16", "int32", "uint16", "float8_e4m3fn_x4", "uint8"

SCRATCH = {"ps": ("psum", [128, 4096], F32)}
for _n, _w, _d in [
        ("X", 1344, BF), ("U", 512, BF), ("V", 512, BF), ("E", 1040, BF), ("Z", 1280, BF),
        ("Y0", 1280, BF), ("Y1", 1280, BF), ("Xh", 960, BF), ("Dh", 1280, BF), ("IL", 640, BF), ("alt", 640, BF),
        ("qu", 128, Q4), ("su", 128, U8), ("qur", 128, Q4), ("sur", 128, U8), ("qv", 128, Q4), ("sv", 128, U8),
        ("qe", 512, Q4), ("se", 512, U8), ("qw", 512, Q4), ("sw", 512, U8), ("qz", 320, Q4), ("sz", 320, U8),
        ("qx0", 336, Q4), ("sx0", 336, U8), ("qx1", 336, Q4), ("sx1", 336, U8), ("qx2", 336, Q4), ("sx2", 336, U8),
        ("qx3", 336, Q4), ("sx3", 336, U8),
        ("lq0", 320, Q4), ("ls0", 320, U8), ("lq1", 320, Q4), ("ls1", 320, U8), ("lq2", 320, Q4), ("ls2", 320, U8),
        ("ones", 128, BF), ("ident", 128, BF),
        ("pi", 8, I32), ("pf", 8, F32), ("rep", 8, I32), ("repu", 8, U16),
        ("wf", 48, F32), ("wi", 16, I32), ("toff", 6, U16),
        ("iota", 320, F32), ("jm", 320, F32), ("tabk", 320, F32), ("cpat", 320, F32), ("delta", 320, BF),
        ("nio", 320, F32), ("r32", 256, F32), ("mask", 128, F32), ("segz", 128, F32), ("kc", 20, F32), ("kc5", 8, F32),
        ("ioff", 2, F32), ("crow", 32, F32), ("tg", 648, BF), ("tn", 648, BF), ("cap", 320, BF), ("hpat", 80, BF),
        ("d42", 256, BF), ("rev", 1024, F32), ("bins", NV, F32), ("t1", 3 * 48, F32), ("tt", NV, F32), ("tv", NV * NV, F32),
        ("TT", 640, F32), ("t16", 80, F32), ("bits", 80, BF), ("hs", 80, F32), ("a16", 20, U16), ("arow", 320, F32),
        ("junk", 20 * NA, BF), ("cmp", 20 * ND, BF), ("acc", 20, F32), ("sc", 20 * HD, F32), ("e16", 20, U16),
        ("gg", 320, BF), ("mx", 324, BF), ("neg", 320, BF),
        ("sm", 4, F32), ("eq", 640, BF), ("cb", 320, BF), ("tc", 320, BF), ("cm", 320, BF),
        ("thr", 4, F32), ("cc", 2 * NP, BF), ("cs", NP, BF), ("pacc", 2, F32), ("p8", 8, U16), ("p16", 6, U16),
        ("p16s", 4, F32), ("a8", 80, F32), ("hrow", 64, F32), ("hm", 128, F32), ("hx", 128, F32), ("key", 12, F32),
        ("keyl", 12, F32), ("nrow", 64, F32), ("valk", 64, F32), ("prow", 64, F32), ("ini", 1, F32), ("val", 320, F32),
        ("yy", 320, F32), ("ext", 320, F32), ("v1", 72, F32), ("pm", 72, U16),
        ("pml", 72, U16), ("pmw", 64, F32), ("yb", 256, BF), ("yc", 256, BF), ("ys", 256, F32), ("voff", 128, U16),
        ("junk4", 16 * VA, BF), ("vg", 32 * VD, F32), ("vs", 8 * VD, F32), ("dd", 4, F32),
        ("doff", 2, U16), ("score", 32, F32), ("best", 2, F32), ("soff", 2, U16), ("zoff", 32, U16),
        ("olr", 320, F32), ("yo", 320, F32)]:
    SCRATCH[_n] = ("sbuf", [128, _w], _d)

DMAS = ["dx", "dx2", "du", "dv", "dwc", "dws", "doc", "dos", "dol", "dya", "dyb"]
SEMAPHORES = ["vec", "act", "pe", "pool", "snd"] + DMAS + [a + str(t) for t in range(R) for a in ("aq", "ak", "ap")]


def rank_program(g, core, T, topo):
    rank = T.rank_of(core)
    if rank is None:
        return
    n_ranks = len(T.cores)
    A, AF = AluOpType, ActivationFunctionType
    queue = {"vec": g.vector, "act": g.scalar, "pe": g.tensor, "pool": g, "sync": g.sync}
    ops = []

    def v(name, a=0, b=None, s=1):
        return (name, a, SCRATCH[name][1][1] if b is None else b, s)

    def col(name, j):
        return (name, j, j + 1, 1)

    def ind(win, off):
        return ("ind", win, off)

    def ap(o):
        if not isinstance(o, tuple):
            return o
        if o[0] == "ind":
            return ap(o[1]).indirect(ap(o[2]))
        return T[o[0]][:, o[1]:o[2]:o[3]] if o[3] != 1 else T[o[0]][:, o[1]:o[2]]

    def parts(os_):
        out = []
        for o in os_:
            if isinstance(o, tuple):
                out += [o[1], o[2]] if o[0] == "ind" else [o]
        return out

    def op(q, fn, reads, writes, sem=None, inc=1):
        ops.append({"q": q, "fn": fn, "r": parts(reads), "w": parts(writes), "sem": sem or q, "inc": inc})

    def ts(out, in0, s1, op0, s2=None, op1=None):
        if op1 is None:
            op("vec", lambda: g.vector.tensor_scalar(ap(out), ap(in0), ap(s1), None, op0), [in0, s1], [out])
        else:
            op("vec", lambda: g.vector.tensor_scalar(ap(out), ap(in0), ap(s1), ap(s2), op0, op1), [in0, s1, s2], [out])

    def tt(out, in0, in1, o):
        op("vec", lambda: g.vector.tensor_tensor(ap(out), ap(in0), ap(in1), o), [in0, in1], [out])

    def cp(out, in_):
        if out[0] == "ind":
            op("vec", lambda: g.vector.tensor_copy(ap(out), ap(in_)), [in_, out[2]], [out[1]])
        else:
            op("vec", lambda: g.vector.tensor_copy(ap(out), ap(in_)), [in_], [out])

    def scan(out, d0, d1, init, op0, op1):
        op("vec", lambda: g.vector.tensor_tensor_scan(ap(out), ap(d0), ap(d1), ap(init), op0, op1), [d0, d1, init], [out])

    def fill(out, c):
        op("vec", lambda: g.vector.memset(ap(out), c), [], [out])

    def quant(q, s, a, b, tile, first=None):
        src = v(tile, 4 * a, 4 * b) if first is None else v(tile, first, first + 4 * (b - a))
        op("vec", lambda: g.vector.quantize_mx(ap(v(q, a, b)), ap(v(s, a, b)), ap(src)), [src], [v(q, a, b), v(s, a, b)])

    def turn(out, in_):
        op("vec", lambda: g.vector.transpose(ap(out), ap(in_)), [in_], [out])

    def act(out, in_, f, bias=0.0, scale=1.0, accum=None):
        if f == AF.Copy and scale == 1.0:
            op("act", lambda: g.scalar.activation(ap(out), ap(in_), f), [in_], [out])
        elif f == AF.Copy:
            op("act", lambda: g.scalar.activation(ap(out), ap(in_), f, scale=scale), [in_], [out])
        elif accum is None:
            op("act", lambda: g.scalar.activation(ap(out), ap(in_), f, bias=ap(bias), scale=scale), [in_, bias], [out])
        else:
            op("act", lambda: g.scalar.activation(ap(out), ap(in_), f, bias=ap(bias), scale=scale, accum_out=ap(accum)),
               [in_, bias], [out, accum])

    def bank(k, a, b):
        return ("ps", 512 * k + a, 512 * k + b, 1)

    def mm(k, wq, ws, w0, xq, xs, a, b):
        o = [v(wq, w0, w0 + 128), v(ws, w0, w0 + 128), v(xq, a, b), v(xs, a, b)]
        op("pe", lambda: g.tensor.matmul_mx(ap(bank(k, 0, b - a)), ap(o[0]), ap(o[1]), ap(o[2]), ap(o[3]), True, True),
           o, [bank(k, 0, b - a)])

    def iota(out, pattern, base, mult=0):
        if SCRATCH[out[0]][2] == I32:
            op("pool", lambda: g.iota(ap(out), pattern, base, mult), [], [out])
        else:
            op("pool", lambda: g.iota(ap(out), pattern, base, mult, allow_small_or_imprecise_dtypes=True), [], [out])

    def dma(q, sem, out, in_, reads, writes):
        op(q, lambda: queue[q].dma_start(out(), in_()), reads, writes, sem=sem, inc=16)

    sent = [0]

    def send(dst, out, in_, sem, codes=False):
        rid, pid = topo.addr(dst)[:2]
        m = topo.mask(core, dst)
        sent[0] += len(topo.engines(core, dst))
        if codes:
            op("pool", lambda: g.remote_dma(ap(out).bitcast(dt.uint8), ap(in_).bitcast(dt.uint8), T.sem[sem], T.sem["snd"],
                                            pid, rid, m), [in_], [], sem="none")
        else:
            op("pool", lambda: g.remote_dma(ap(out), ap(in_), T.sem[sem], T.sem["snd"], pid, rid, m), [in_], [], sem="none")

    def arrive(src, sem, writes):
        op(None, None, [], writes, sem=sem, inc=len(writes) * len(topo.engines(src, core)))

    dma("act", "du", lambda: ap(v("U")), lambda: T.u[:], [], [v("U")])
    dma("sync", "dx", lambda: ap(v("X", 0, 1280)), lambda: T.x[:], [], [v("X", 0, 1280)])
    dma("act", "dx2", lambda: ap(v("X", 1280, 1344)), lambda: T.x[:, 0:64], [], [v("X", 1280, 1344)])
    dma("sync", "dwc", lambda: ap(v("qw")).bitcast(dt.uint8), lambda: T.wc[:], [v("X", 0, 2)], [v("qw")])
    dma("sync", "dws", lambda: ap(v("sw")), lambda: T.ws[:], [], [v("sw")])
    dma("sync", "dv", lambda: ap(v("V")), lambda: T.v[:], [], [v("V")])

    a_col, n_col, q4_col, h_col = col("pf", 0), col("pf", 1), col("pf", 2), col("pf", 3)
    w = [v("wf", 8 * i, 8 * i + 5) for i in range(6)]
    wi = [v("wi", 8 * i, 8 * i + 5) for i in range(2)]
    t1 = [v("t1", 48 * i, 48 * i + NV) for i in range(3)]
    iota(col("pi", 0), [[0, 1]], 0, 1)
    fill(v("ones"), 1.0)
    op("pool", lambda: g.affine_select(ap(v("ident")), ap(v("ones")), [[-1, 128]], A.is_equal, 0.0, 0, 1),
       [v("ones")], [v("ident")])
    iota(v("bins", 1, 41), [[0, 2], [1, 20]], 0)
    iota(w[0], [[64, 5]], 0)
    iota(v("rep"), [[16, 8]], 0)
    fill(v("E"), 0.0)
    act(v("E", 2, 514, 4), v("ident"), AF.Copy)
    act(v("E", 523, 1035, 4), v("ident"), AF.Copy)
    for j, bit in enumerate((15, 3, 12, 16)):
        ts(col("pi", 4 + j), col("pi", 0), bit, A.bitwise_and)
    fill(v("bins", 0, NV, NV - 1), -1.0)
    cp(v("pf", 0, 4), v("pi", 4, 8))
    fill(v("hpat"), 2.0)
    ts(t1[1], v("bins"), a_col, A.subtract, 16.0, A.is_equal)
    ts(t1[0], v("bins"), a_col, A.is_equal)
    ts(t1[2], t1[1], 1024.0, A.mult)
    ts(col("pf", 4), q4_col, 4.0, A.mult, h_col, A.subtract)
    tt(v("tt"), t1[0], t1[2], A.add)
    ts(w[1], w[0], col("pf", 4), A.add)
    fill(v("hpat", 1, 80, 4), 0.0)
    ts(w[2], w[1], 0.0, A.is_lt, 320.0, A.mult)
    cp(v("repu"), v("rep"))
    iota(v("iota"), [[1, 320]], 0)
    iota(v("r32", 0, 128), [[0, 4], [1, 32]], 0)
    iota(v("tg", 0, 128), [[-1, 128]], -1)
    iota(v("tg", 128, 384), [[-1, 256]], 256)
    iota(v("tg", 384, 648), [[0, 264]], 1)
    tt(wi[0], w[1], w[2], A.add)
    fill(v("segz"), 1.0)
    for i in range(21):
        act(v("tv", NV * i, NV * i + NV), v("tt"), AF.Identity, bias=col("tt", i))
    ts(wi[1], wi[0], 16, A.bitwise_and)
    ts(w[3], wi[0], h_col, A.add, n_col, A.add)
    ts(col("pf", 5), a_col, -1.0, A.mult, -15.0 / 16, A.add)
    ts(w[4], wi[1], 19.0, A.mult)
    ts(col("pf", 6), a_col, 0.5, A.add)
    tt(w[5], w[4], w[3], A.add)
    ts(col("pf", 7), a_col, BIG, A.mult)
    cp(v("toff", 0, 5), w[5])
    fill(v("segz", 0, 128, 32), 0.0)
    for b, first in enumerate((2, 522, 0, 520)):
        quant("qe", "se", 128 * b, 128 * b + 128, "E", first)
    quant("qu", "su", 0, 128, "U")
    fill(v("tn", 0, 128), 1.0)
    op("vec", lambda: g.vector.tensor_copy(ap(v("qur")).bitcast(dt.uint32),
                                           ap(v("qu")).bitcast(dt.uint32).indirect(ap(v("repu")))),
       [v("qu"), v("repu")], [v("qur")])
    act(v("sur"), ind(v("su"), v("repu")), AF.Copy)
    act(v("tv", NV * 21, NV * 41), v("tv", NV, NV * 21), AF.Copy)
    act(v("tv", NV * 41, NV * 42), v("tt"), AF.Copy)
    act(v("r32", 128, 256), v("r32", 0, 128), AF.Abs, bias=col("pf", 5))
    act(v("pmw"), v("iota", 0, 64), AF.Copy, scale=0.0)
    act(v("mask"), v("r32", 128, 256), AF.Relu, bias=8.5, scale=-8.0)
    quant("qx0", "sx0", 0, HA, "X")
    quant("qx0", "sx0", HA, 336, "X")
    fill(v("tn", 128, 648), 0.0)

    for t in range(R):
        qx, sx, lq, ls = "qx%d" % t, "sx%d" % t, "lq%d" % t, "ls%d" % t
        reader = T.cores[(rank - STEP[t]) % n_ranks]
        partner = T.cores[(rank + STEP[t]) % n_ranks]
        y_old, y_new = ("Y0", "Y1") if t % 2 == 0 else ("Y1", "Y0")

        def half_x(b):
            out = v("Xh", C * b, C * b + C) if b < 3 else v("IL", 0, 640, 2)
            if t == 0:
                act(out, v("X", b, 1280, 4), AF.Copy, scale=0.5)
            else:
                act(out, v(y_old, C * b, C * b + C), AF.Copy, scale=1.0 / 64)

        mm(0, "qu", "su", 0, qx, sx, 0, HA)
        mm(7, "qu", "su", 0, qx, sx, 160, 336)
        mm(1, "qur", "sur", 0, qx, sx, 0, NA)
        mm(2, "qur", "sur", 0, qx, sx, NA, C)
        send(reader, v(lq), v(qx, 0, C), "aq%d" % t, codes=True)
        send(reader, v(ls), v(sx, 0, C), "aq%d" % t)
        arrive(partner, "aq%d" % t, [v(lq), v(ls)])
        if t == 0:
            iota(v("kc5", 4, 8), [[16, 4]], 0)
            iota(v("cap"), [[0, C]], K)
            iota(v("val"), [[0, C]], 0)
            iota(v("tabk"), [[16 - int(KK), 20], [1, 16]], 20 * int(KK))
            iota(v("jm"), [[0, 20], [1, 16]], 0)
            iota(v("kc"), [[int(KK), 20]], -20 * int(KK))
            iota(v("d42"), [[0, 128], [NV, 2]], 0)
        for h, k in enumerate((0, 7)):
            turn(v("TT", 160 * h, 160 * h + 160), bank(k, 0, 160))
            turn(v("TT", C + 160 * h, C + 160 * h + 160), bank(k, 16, 176))
        cp(v("t16"), ind(v("TT"), v("toff", 0, 5)))
        for b in range(4):
            mm(3 + b, "qe", "se", 128 * b, lq, ls, 0, C)

        def sums(k):
            scan(v("sc", HD * k, HD * k + HD), v("cmp", ND * k, ND * k + HD), v("cmp", ND * k + HD, ND * k + ND),
                 col("acc", k), A.add, A.add)
        lag = 3
        for k in range(20):
            act(v("junk", NA * k, NA * k + NA), bank(1, 0, NA), AF.Sign, bias=col("t16", 4 * k), scale=-1.0,
                accum=col("acc", k))
            ts(v("cmp", ND * k, ND * k + ND), bank(2, 0, ND), col("t16", 4 * k), A.is_gt, -2.0, A.mult)
            if k == 0:
                ts(v("bits"), v("t16"), 0.0, A.is_gt)
            if k == 1:
                scan(v("hs"), v("hpat"), v("bits"), 0.0, A.mult, A.add)
            if k == 2:
                cp(v("a16"), v("hs", 3, 80, 4))
            if k >= lag:
                sums(k - lag)
        for k in range(20 - lag, 20):
            sums(k)
        ts(v("e16"), v("sc", HD - 1, 20 * HD, HD), -1.0, A.mult, float(NA), A.add)

        n_top = col("sm", 3)
        act(v("neg"), ind(v("tn"), v("e16")), AF.Identity, accum=n_top)
        cp(v("gg"), ind(v("tg"), v("e16")))
        act(v("arow"), ind(v("iota"), v("a16")), AF.Copy, scale=40.0)
        if t == 0:
            act(v("kc5", 0, 4), v("kc5", 4, 8), AF.Identity, bias=col("pf", 6))
        half_x(0)
        half_x(1)
        g_max, g_min, few, g_cut = col("mx", 159), col("mx", 319), col("mx", 320), col("mx", 322)
        scan(v("mx", 160, 320), v("gg", 0, 160), v("gg", 160, 320), BIG, A.min, A.min)
        ts(few, n_top, K - 0.5, A.is_lt, 4096.0, A.mult)
        scan(v("mx", 0, 160), v("gg", 0, 160), v("gg", 160, 320), -BIG, A.max, A.max)
        ts(v("eq", C, 2 * C), v("gg"), few, A.subtract, g_min, A.is_equal)
        ts(g_cut, few, g_min, A.add, g_max, A.min)
        scan(v("cb"), v("neg"), v("eq", C, 2 * C), 0.0, A.add, A.subtract)
        ts(v("eq", 0, C), v("gg"), g_cut, A.is_equal)
        ts(v("thr"), v("kc5", 0, 4), col("cb", C - 1), A.add)
        scan(v("tc"), v("eq", 0, C), v("cap"), col("cb", C - 1), A.add, A.min)
        scan(v("cm"), v("cb"), v("tc"), BIG, A.min, A.add)

        hp = NP // 2
        for k in range(2):
            ts(v("cc", NP * k, NP * k + NP), v("cm", 16 * k, 16 * k + NP), col("thr", k), A.is_lt)
            act(v("junk", C * k, C * k + C - 32), v("cm", 32, C), AF.Sign, bias=col("thr", 2 + k),
                scale=-1.0, accum=col("pacc", k))
        for k in range(2):
            scan(v("cs", hp * k, hp * k + hp), v("cc", NP * k, NP * k + hp), v("cc", NP * k + hp, NP * k + NP),
                 16.0 * k - hp, A.add, A.add)
        ts(v("p8", 0, 2), v("cs", hp - 1, NP, hp), float(hp), A.add)
        ts(col("p8", 2), col("cs", NP - 1), float(hp), A.add)
        ts(col("p8", 7), col("cs", hp - 1), float(hp), A.add)
        ts(v("p8", 3, 6, 2), v("pacc"), 0.5, A.mult, (C + 32) / 2.0, A.add)
        ts(v("p8", 4, 7, 2), v("pacc"), 0.5, A.mult, (C + 32) / 2.0, A.add)

        pk = v("p16", 0, 4)
        tt(v("hm"), ind(v("arow"), v("p8")), v("mask"), A.mult)
        ts(v("p16s"), v("p8", 0, 8, 2), 1.0 / 16, A.mult)
        scan(v("hx"), v("segz"), v("hm"), 0.0, A.mult, A.add)
        cp(pk, v("p8", 0, 8, 2))
        key, keyl = v("key", 4 * t, 4 * t + 4), v("keyl", 4 * t, 4 * t + 4)
        tt(key, v("hx", 31, 128, 32), v("p16s"), A.add)
        send(reader, keyl, key, "ak%d" % t)
        arrive(partner, "ak%d" % t, [keyl])
        cp(col("p16", 4), col("p8", 0))
        if t == 0:
            iota(v("alt"), [[0, C], [1, 2]], 0)

        act(v("valk"), ind(v("tabk"), pk), AF.Copy)
        act(v("prow"), ind(v("iota"), pk), AF.Copy)
        act(v("a8"), ind(v("arow"), v("p16", 0, 5)), AF.Copy, scale=8.0)
        if t == 0:
            act(v("nio"), v("iota"), AF.Identity, bias=129.0 + 20.0 - 0.5 + 1.0 / 32, scale=-1.0 / 16)
            act(v("cpat"), v("jm"), AF.Relu, bias=col("pf", 7), scale=-BIG)
            fill(v("delta"), 0.0)
            fill(v("delta", 16, 320, 16), -KK)
        for b in range(4 if t else 2):
            act(v("Dh", C * b, C * b + C), bank(3 + b, 0, C), AF.Copy, scale=0.5)
        cp(ind(v("val"), pk), v("valk"))
        ts(v("ini"), col("prow", K - 1), 20 * KK - C, A.add)
        tt(v("hrow"), ind(v("arow"), pk), v("a8", 1, 65), A.add)
        scan(v("yy"), v("delta"), v("val"), v("ini"), A.add, A.max)
        tt(v("nrow"), ind(v("nio"), pk), v("hrow"), A.subtract)
        scan(v("ext"), v("yy"), v("cpat"), BIG, A.min, A.max)
        v1, v2, v3 = v("v1", 0, 20), v("v1", 24, 44), v("v1", 48, 68)
        pm, pml = v("pm", 24 * t, 24 * t + 20), v("pml", 24 * t, 24 * t + 20)
        tt(v1, v("ext", 15, 320, 16), v("kc"), A.add)

        for k in range(2):
            ts(v("yb", K * k, K * k + K), v("nrow"), col("keyl", 4 * t + k), A.add)
            act(v("yb", K * (k + 2), K * (k + 3)), v("nrow"), AF.Identity, bias=col("keyl", 4 * t + k + 2))
        ts(v2, v1, 0.0, A.is_lt, float(C), A.mult)
        ts(v("yc"), v("yb"), 128.0, A.max, 127.0 + NV, A.min)
        tt(v3, v1, v2, A.add)
        scan(v("ys"), v("d42"), v("yc"), 0.0, A.mult, A.add)
        cp(pm, v3)
        send(reader, pml, pm, "ap%d" % t)
        arrive(partner, "ap%d" % t, [pml])
        if t == 0:
            iota(v("rev", 512, 1024), [[-32, 512]], 32 * 511)
            act(v("rev", 0, 512), v("rev", 512, 1024), AF.Identity, bias=32.0 * 512)
        ts(v("voff"), v("ys", 1, 256, 2), 128.0 * (NV + 1), A.subtract)
        v_act = col("dd", 3)
        act(v("junk4"), ind(v("tv"), v("voff", 0, VA)), AF.Identity, accum=v_act)
        if t == 0:
            ops.append(ops.pop(-3))
        cp(v("vg", 0, 16 * VD), ind(v("tv"), v("voff", VA, VA + VD)))
        tt(v("vg", 16 * VD, 32 * VD), ind(v("tv"), v("voff", VA + VD, 128)), v("vg", 0, 16 * VD), A.add)
        scan(v("vs"), v("vg", 16 * VD, 24 * VD), v("vg", 24 * VD, 32 * VD), -511.5, A.add, A.add)
        if t == 0:
            act(v("crow"), v("iota", 0, 32), AF.Identity, bias=15.5, scale=-1.0)
            act(v("ioff"), v("kc5", 0, 2), AF.Identity, bias=15.0)
            act(v("Dh", C * 3, C * 4), bank(6, 0, C), AF.Copy, scale=0.5)
        half_x(3)
        if t == 0:
            act(v("Dh", C * 2, C * 3), bank(5, 0, C), AF.Copy, scale=0.5)
        else:
            half_x(2)
        last = col("vs", 8 * VD - 1)
        m_hi, m_lo = 1.5 * 2.0 ** 33, 1.5 * 2.0 ** 28
        ts(col("dd", 0), v_act, last, A.add, m_hi, A.add)
        ts(col("dd", 1), v_act, last, A.add, 511.5, A.subtract)
        ts(col("doff", 1), col("dd", 0), m_hi + 1023.0 * 1024, A.subtract, -1.0 / 1024, A.mult)
        ts(col("doff", 0), col("dd", 0), m_hi, A.subtract, col("dd", 1), A.subtract)
        tt(v("score"), ind(v("rev"), v("doff")), v("crow"), A.add)
        op("vec", lambda: g.vector.tensor_reduce(ap(col("best", 0)), ap(v("score")), AxisListType.X, A.max),
           [v("score")], [col("best", 0)])
        cp(v("pmw", 0, 20), pml)
        ts(col("best", 1), col("best", 0), m_lo, A.add, m_lo, A.subtract)
        cp(v("pmw", 20, 40), pml)
        ts(v("soff"), v("ioff"), col("best", 0), A.subtract, col("best", 1), A.add)
        cp(v("zoff"), ind(v("pmw"), v("soff")))

        zo = v("zoff", 0, 20)
        act(v("IL", 1, 640, 2), ind(v("Dh", 3 * C, 4 * C), zo), AF.Copy)
        if t == 0:
            half_x(2)
        for b in (0, 3, 2, 1):
            if b == 3:
                scan(v("Z", 1, 1280, 2), v("alt"), v("IL"), 0.0, A.mult, A.add)
            else:
                tt(v("Z", b, 1280, 4), ind(v("Dh", C * b, C * b + C), zo), v("Xh", C * b, C * b + C), A.add)
        if t == 0:
            for b in range(4):
                act(v("Y0", C * b, C * b + C), v("X", b, 1280, 4), AF.Copy, scale=32.0)
        if t < R - 1:
            iota(v("val"), [[0, C]], 0)
        else:
            act(v("olr"), ind(v("iota"), zo), AF.Copy)
            dma("sync", "dol", lambda: T.ol[:], lambda: T["olr"][0:128:16, :], [v("olr")], [])
        runs = ((0, HA), (HA, C))
        for c0, c1 in runs:
            quant("qz", "sz", c0, c1, "Z")
        for h, (c0, c1) in enumerate(runs):
            for b in range(4):
                mm(4 * h + b, "qw", "sw", 128 * b, "qz", "sz", c0, c1)
        if t == 0:
            quant("qv", "sv", 0, 128, "V")
        qn, sn = "qx%d" % (t + 1), "sx%d" % (t + 1)
        for h, (c0, c1) in enumerate(runs):
            for b in range(4):
                y_run = v(y_new, C * b + c0, C * b + c1)
                tt(y_run, bank(4 * h + b, 0, c1 - c0), v(y_old, C * b + c0, C * b + c1), A.add)
                if 4 * h + b < 6:
                    act(v("X", 4 * c0 + b, 4 * c1, 4), y_run, AF.Copy, scale=1.0 / 32)
        for b in (2, 3):
            ts(v("X", 4 * HA + b, 1280, 4), v(y_new, C * b + HA, C * b + C), 1.0 / 32, A.mult)
        if t < R - 1:
            cp(v("X", 1280, 1344), v("X", 0, 64))
        quant(qn, sn, 0, HA, "X")
        quant(qn, sn, HA, 336 if t < R - 1 else C, "X")

    mm(0, "qv", "sv", 0, "qx3", "sx3", 0, HA)
    mm(1, "qv", "sv", 0, "qx3", "sx3", HA, C)
    dma("sync", "doc", lambda: T.oc[:], lambda: ap(v("qx3", 0, C)).bitcast(dt.uint8), [v("qx3", 0, C)], [])
    act(v("yo", 0, HA), bank(0, 0, HA), AF.Copy)
    dma("act", "dya", lambda: T.y[:, 0:HA], lambda: ap(v("yo", 0, HA)), [v("yo", 0, HA)], [])
    for k in range(4):
        dma("act" if k % 2 else "sync", "dos", lambda k=k: T.osc[4 * k:4 * k + 4, :],
            lambda k=k: T["sx3"][32 * k:32 * k + 4, 0:C], [v("sx3", 0, C)], [])
    cp(v("yo", HA, C), bank(1, 0, C - HA))
    dma("sync", "dyb", lambda: T.y[:, HA:C], lambda: ap(v("yo", HA, C)), [v("yo", HA, C)], [])

    def cover(o):
        m = np.zeros(SCRATCH[o[0]][1][1], bool)
        if o[0] == "ps":
            m[o[1] // 512 * 512:o[1] // 512 * 512 + 512] = True
        else:
            m[o[1]:o[2]:o[3]] = True
        return m

    touched, order, known = {}, {}, {}
    for i, o in enumerate(ops):
        deps = set()
        acc = [(x, False) for x in o["r"]] + [(x, True) for x in o["w"]]
        for x, wr in acc:
            m = cover(x)
            for j, mj, wj in touched.get(x[0], []):
                clash = wr or wj or (x[0] == "ps" and ops[j]["q"] != o["q"])
                if clash and ops[j]["sem"] != "none" and (m & mj).any():
                    deps.add(j)
        for x, wr in acc:
            touched.setdefault(x[0], []).append((i, cover(x), wr))
        o["pos"] = order[o["sem"]] = order.get(o["sem"], 0) + 1
        seen = known.setdefault(o["q"], {}) if o["q"] else {}
        o["waits"] = []
        for j in sorted(deps, reverse=True):
            d = ops[j]
            if o["q"] and seen.get(d["sem"], 0) < d["pos"]:
                o["waits"].append(j)
                d["needed"] = True
                for s, p in d["clock"].items():
                    seen[s] = max(seen.get(s, 0), p)
        o["clock"] = dict(seen)
        o["clock"][o["sem"]] = o["pos"]

    count = {}
    for o in ops:
        if o["q"]:
            for j in o["waits"]:
                queue[o["q"]].wait_ge(T.sem[ops[j]["sem"]], ops[j]["count"])
        call = o["fn"]() if o["fn"] else None
        if o["sem"] != "none" and (o.get("needed") or o["inc"] > 1):
            o["count"] = count[o["sem"]] = count.get(o["sem"], 0) + o["inc"]
            if call is not None:
                call.then_inc(T.sem[o["sem"]], o["inc"])
    g.wait_ge(T.sem["snd"], sent[0])
    for s in ("dol", "doc", "dos", "dya", "dyb"):
        g.wait_ge(T.sem[s], count[s])
